import numpy as np
import ml_dtypes


def mxq(x, axis, fmt="e4m3"):
    dtype, down = {"e4m3": (ml_dtypes.float8_e4m3fn, 7), "e5m2": (ml_dtypes.float8_e5m2, 14)}[fmt]
    v = np.moveaxis(np.asarray(x, np.float32).astype(ml_dtypes.bfloat16).astype(np.float64), axis, -1)
    blocks = v.reshape(v.shape[:-1] + (-1, 32))
    amax = np.abs(blocks).max(-1, keepdims=True)
    byte = np.maximum(np.where(amax > 0, np.frexp(amax)[1] - 1 + 127, 0) - down, 1)
    scale = np.exp2(byte - 127.0)
    codes = (blocks / scale).astype(np.float32).astype(dtype).astype(np.float64)
    return np.moveaxis((codes * scale).reshape(v.shape), -1, axis)


WIDE = False


def mx_kscale(k):
    if not WIDE:
        return np.ones(k)
    levels = np.array([18, -18])
    if k % 512:
        return np.exp2(np.random.permutation(np.resize(levels, k // 32))).repeat(32)
    a = np.empty((k // 512, 16))
    for p in range(k // 512):
        a[p, :8] = np.random.permutation(np.resize(levels, 8))
        for g in range(8):
            far = levels[np.abs(levels - a[p, g]) >= 10]
            a[p, g + 8] = far[np.random.randint(len(far))]
    return np.exp2(a.ravel()).repeat(32)


def f64(x):
    return np.asarray(x).astype(np.float64)


def striped(idx):
    return np.tile(np.asarray(idx).reshape(-1, 16).T, (8, 1)).astype(np.uint16)


def unstriped(offs):
    return offs[:16].T.reshape(-1).astype(np.int64)


E2M1 = np.array([0.0, 0.5, 1.0, 1.5, 2.0, 3.0, 4.0, 6.0, -0.0, -0.5, -1.0, -1.5, -2.0, -3.0, -4.0, -6.0])


def pack_weight(w, fmt):
    k, n = w.shape
    w = f64(np.asarray(w, np.float32).astype(ml_dtypes.bfloat16)).reshape(k // 32, 32, n)
    amax = np.abs(w).max(1)
    if fmt == "e4m3":
        byte = np.frexp(amax)[1] - 1 + 127 - 7
    else:
        mant, ex = np.frexp(amax / 6.0)
        byte = np.where(mant > 0.5, ex, ex - 1) + 127
    byte = np.clip(np.where(amax > 0, byte, 1), 1, 254)
    scaled = (w * np.exp2(127.0 - byte)[:, None, :]).reshape(k, n).astype(np.float32)
    by_word = np.ascontiguousarray(scaled.reshape(k // 512, 128, 4, n).transpose(0, 1, 3, 2))
    if fmt == "e4m3":
        words = by_word.astype(ml_dtypes.float8_e4m3fn).view(np.uint8)
    else:
        c = by_word.astype(ml_dtypes.float4_e2m1fn).view(np.uint8) & 0xF
        words = (c[..., 0::2] | (c[..., 1::2] << 4)).reshape(k // 512, 128, 2 * n)
    return np.ascontiguousarray(words), np.ascontiguousarray(byte.astype(np.uint8).reshape(k // 512, 16, n))


def unpack_weight(words, scales, fmt):
    g, _, n = scales.shape
    words = np.ascontiguousarray(words).reshape(g, 128, n, -1)
    if fmt == "e4m3":
        vals = words.view(ml_dtypes.float8_e4m3fn).astype(np.float64)
    else:
        nib = np.empty((g, 128, n, 4), np.uint8)
        nib[..., 0::2] = words & 0xF
        nib[..., 1::2] = words >> 4
        vals = E2M1[nib]
    vals = vals * np.repeat(np.exp2(scales.astype(np.float64) - 127.0), 8, axis=1)[..., None]
    return vals.transpose(0, 1, 3, 2).reshape(g * 512, n)


def planes(y):
    n, m = y.shape
    v = y.astype(np.float32).astype(ml_dtypes.bfloat16).astype(np.float64).reshape(n // 32, 32, m)
    top = np.abs(v).max(1)
    byte = np.clip(np.where(top > 0, np.frexp(top)[1] - 1 + 127 - 7, 1), 1, 254)
    codes = (v * np.exp2(127.0 - byte)[:, None, :]).reshape(n, m).astype(np.float32).astype(ml_dtypes.float8_e4m3fn).view(np.uint8)
    words = codes.reshape(n // 512, 128, 4, m).transpose(0, 1, 3, 2)
    return np.ascontiguousarray(words), np.ascontiguousarray(byte.astype(np.uint8).reshape(n // 512, 16, m))


def setup_inputs():
    n = np.random.standard_normal
    uni = np.random.uniform
    ord_ = np.random.permutation(512)
    nx = np.roll(ord_, -1)[np.argsort(ord_)]
    f_m = mx_kscale(512)
    W_ = pack_weight(n((512, 512)) / np.sqrt(512) * f_m[:, None], "e4m3")
    return {
        "W_words": W_[0],
        "W_scales": W_[1],
        "dyT": (n((512, 512)) / f_m[:, None]).astype(np.float32),
        "mu": (uni(0.2, 0.8, (512, 1))).astype(np.float32),
        "offs": striped(nx),
    }


def reference(W_words, W_scales, dyT, mu, offs):
    nx = unstriped(offs)
    W = unpack_weight(W_words, W_scales, "e4m3")
    u = W.T @ mxq(f64(dyT), 0, "e5m2")
    un = u[:, nx]
    out_0 = f64(mu) * u + (1.0 - f64(mu)) * un
    return (out_0,) + planes(out_0)

@@ -1,0 +1,163 @@
+from contextlib import ExitStack
+
+import concourse.mybir as mybir
+
+F32 = mybir.dt.float32
+BF16 = mybir.dt.bfloat16
+I32 = mybir.dt.int32
+U8 = mybir.dt.uint8
+U16 = mybir.dt.uint16
+E4M3X4 = mybir.dt.float8_e4m3fn_x4
+E5M2X4 = mybir.dt.float8_e5m2_x4
+MULT = mybir.AluOpType.mult
+ADD = mybir.AluOpType.add
+COPY = mybir.ActivationFunctionType.Copy
+
+P = 128
+LANES = 4
+X = 512
+D = 512
+CHUNK = 128
+HALF = 256
+PER_COL = 16
+RUN = 4
+
+FLOPS = 2 * 512 * 512 * 512
+
+
+def tile_attend_gtshift_pl_kernel(tc, W_words, W_scales, dyT, mu, offs, out_0, out_1, out_2):
+    nc = tc.nc
+    chunks = X // CHUNK
+
+    def interleave(engine_copy, dst, src):
+        engine_copy(
+            dst.rearrange("p (c i) t -> p c t i", i=RUN),
+            src.rearrange("p t (c i) -> p c t i", i=RUN),
+        )
+
+    with ExitStack() as ctx:
+        sb = ctx.enter_context(tc.tile_pool(name="sb", bufs=1))
+        ps = ctx.enter_context(tc.psum_pool(name="ps", bufs=1))
+
+        offsets = sb.tile([P, X // PER_COL], U16, name="offsets")
+        ws_raw = sb.tile([P, D], U8, name="ws_raw", align_bytes=64)
+        w_raw = sb.tile([P, D], I32, name="w_raw", align_bytes=64)
+        nc.vector.memset(ws_raw[:].bitcast(I32), 0)
+        nc.sync.dma_start(w_raw[:], W_words[0].rearrange("p n t -> p (n t)").bitcast(I32))
+        for q in range(4):
+            nc.sync.dma_start(
+                ws_raw[32 * q : 32 * q + 4, :].bitcast(I32), W_scales[0, 4 * q : 4 * q + 4, :].bitcast(I32)
+            )
+        dy_view = dyT.rearrange("(p j) x -> p j x", j=LANES)
+        dy_raw = []
+        for c in range(chunks):
+            raw = sb.tile([P, LANES, CHUNK], F32, name=f"dy_raw{c}", align_bytes=64)
+            nc.sync.dma_start(raw[:], dy_view[:, :, c * CHUNK : (c + 1) * CHUNK])
+            dy_raw.append(raw)
+        nc.sync.dma_start(offsets[:], offs)
+        mu_sb = sb.tile([P, LANES], F32, name="mu_sb")
+        nc.sync.dma_start(mu_sb[:], mu.rearrange("(p t) o -> p (t o)", t=LANES))
+
+        w_deal = sb.tile([P, D], I32, name="w_deal", align_bytes=64)
+        nc.vector.tensor_copy(
+            w_deal[:].rearrange("p (t s i) -> p s t i", t=LANES, i=RUN),
+            w_raw[:].rearrange("p (s i t) -> p s t i", t=LANES, i=RUN),
+        )
+        ws_deal = sb.tile([P, D], U8, name="ws_deal", align_bytes=64)
+        nc.vector.tensor_copy(
+            ws_deal[:].rearrange("p (t s) -> p t s", t=LANES),
+            ws_raw[:].rearrange("p (s t) -> p t s", t=LANES),
+        )
+
+        dy_codes = sb.tile([P, X], I32, name="dy_codes", align_bytes=64)
+        dy_scales = sb.tile([P, X], U8, name="dy_scales", align_bytes=64)
+        for c in range(chunks):
+            grouped = sb.tile([P, CHUNK, LANES], BF16, name=f"dy_bf{c}", align_bytes=64)
+            if c == chunks - 1:
+                cut = 80
+                interleave(nc.vector.tensor_copy, grouped[:, :cut, :], dy_raw[c][:, :, :cut])
+                interleave(nc.scalar.copy, grouped[:, cut:, :], dy_raw[c][:, :, cut:])
+            elif c % 2 == 0:
+                interleave(nc.scalar.copy, grouped[:], dy_raw[c][:])
+            else:
+                interleave(nc.vector.tensor_copy, grouped[:], dy_raw[c][:])
+            cols = slice(c * CHUNK, (c + 1) * CHUNK)
+            nc.vector.quantize_mx(
+                out=dy_codes[:, cols].bitcast(E5M2X4),
+                scales=dy_scales[:, cols],
+                in_=grouped[:].rearrange("p c t -> p (c t)"),
+            )
+
+        one_less = sb.tile([P, LANES], F32, name="one_less")
+        nc.vector.tensor_scalar(one_less[:], mu_sb[:], -1.0, 1.0, MULT, ADD)
+
+        banks = []
+        for t in range(LANES):
+            bank = ps.tile([P, X], F32, name=f"bank{t}")
+            nc.tensor.matmul_mx(
+                out=bank[:],
+                lhsT=w_deal[:, t * P : (t + 1) * P].bitcast(E4M3X4),
+                lhsT_scale=ws_deal[:, t * P : (t + 1) * P],
+                rhs=dy_codes[:].bitcast(E5M2X4),
+                rhs_scale=dy_scales[:],
+                start=True,
+                stop=True,
+            )
+            banks.append(bank)
+
+        u = [sb.tile([P, X], F32, name=f"u{t}", align_bytes=64) for t in range(LANES)]
+        own = [sb.tile([P, X], F32, name=f"own{t}", align_bytes=64) for t in range(LANES)]
+        nxt = [sb.tile([P, X], F32, name=f"nxt{t}", align_bytes=64) for t in range(LANES)]
+        y = sb.tile([P, LANES, X], F32, name="y", align_bytes=64)
+        y_view = out_0.rearrange("(p t) x -> p t x", t=LANES)
+
+        def scale_own(t):
+            nc.scalar.activation(own[t][:], banks[t][:], COPY, scale=mu_sb[:, t : t + 1])
+
+        nc.vector.tensor_copy(u[0][:], banks[0][:])
+        nc.scalar.copy(u[1][:], banks[1][:])
+        scale_own(0)
+        scale_own(1)
+        nc.scalar.copy(u[2][:], banks[2][:])
+        scale_own(2)
+        scale_own(3)
+        nc.scalar.copy(u[3][:], banks[3][:])
+
+        def gather(t, a, b):
+            nc.vector.tensor_copy(nxt[t][:, a:b], u[t][:].indirect(offsets[:, a // PER_COL : b // PER_COL]))
+
+        def mix(t, a, b):
+            nc.vector.scalar_tensor_tensor(
+                y[:, t, a:b], nxt[t][:, a:b], one_less[:, t : t + 1], own[t][:, a:b], MULT, ADD
+            )
+
+        for t in range(LANES - 1):
+            gather(t, 0, HALF)
+            gather(t, HALF, X)
+            mix(t, 0, X)
+            nc.sync.dma_start(y_view[:, t, :], y[:, t, :])
+
+        y_codes = sb.tile([P, X], I32, name="y_codes", align_bytes=64)
+        y_scales = sb.tile([P, X], U8, name="y_scales", align_bytes=64)
+        words_view = out_1[0].rearrange("p n t -> p (n t)").bitcast(I32)
+        last = LANES - 1
+        for c in range(chunks):
+            a, b = c * CHUNK, (c + 1) * CHUNK
+            gather(last, a, b)
+            mix(last, a, b)
+            if c % 2 == 1:
+                nc.sync.dma_start(y_view[:, last, b - HALF : b], y[:, last, b - HALF : b])
+            y_bf = sb.tile([P, CHUNK, LANES], BF16, name=f"y_bf{c}", align_bytes=64)
+            interleave(nc.vector.tensor_copy if c == chunks - 1 else nc.scalar.copy, y_bf[:], y[:, :, a:b])
+            nc.vector.quantize_mx(
+                out=y_codes[:, a:b].bitcast(E4M3X4),
+                scales=y_scales[:, a:b],
+                in_=y_bf[:].rearrange("p c t -> p (c t)"),
+            )
+            if c % 2 == 1:
+                nc.sync.dma_start(words_view[:, b - HALF : b], y_codes[:, b - HALF : b])
+        for q in range(4):
+            queue = nc.scalar if q % 2 == 0 else nc.sync
+            queue.dma_start(
+                out_2[0, 4 * q : 4 * q + 4, :].bitcast(I32), y_scales[32 * q : 32 * q + 4, :].bitcast(I32)
+            )

@@ -21,6 +21,7 @@ CHUNK = 128
 HALF = 256
 PER_COL = 16
 RUN = 4
+DY_PIECES = ((0, 128, 0), (128, 384, 160), (384, 512, 80))
 
 FLOPS = 2 * 512 * 512 * 512
 
@@ -43,26 +44,21 @@ def tile_attend_gtshift_pl_kernel(tc, W_words, W_scales, dyT, mu, offs, out_0, o
         ws_raw = sb.tile([P, D], U8, name="ws_raw", align_bytes=64)
         w_raw = sb.tile([P, D], I32, name="w_raw", align_bytes=64)
         nc.vector.memset(ws_raw[:].bitcast(I32), 0)
-        nc.sync.dma_start(w_raw[:], W_words[0].rearrange("p n t -> p (n t)").bitcast(I32))
         for q in range(4):
             nc.sync.dma_start(
                 ws_raw[32 * q : 32 * q + 4, :].bitcast(I32), W_scales[0, 4 * q : 4 * q + 4, :].bitcast(I32)
             )
         dy_view = dyT.rearrange("(p j) x -> p j x", j=LANES)
         dy_raw = []
-        for c in range(chunks):
-            raw = sb.tile([P, LANES, CHUNK], F32, name=f"dy_raw{c}", align_bytes=64)
-            nc.sync.dma_start(raw[:], dy_view[:, :, c * CHUNK : (c + 1) * CHUNK])
+        for a, b, cut in DY_PIECES:
+            raw = sb.tile([P, LANES, b - a], F32, name=f"dy_raw{a}", align_bytes=64)
+            nc.sync.dma_start(raw[:], dy_view[:, :, a:b])
             dy_raw.append(raw)
+        nc.sync.dma_start(w_raw[:], W_words[0].rearrange("p n t -> p (n t)").bitcast(I32))
         nc.sync.dma_start(offsets[:], offs)
         mu_sb = sb.tile([P, LANES], F32, name="mu_sb")
         nc.sync.dma_start(mu_sb[:], mu.rearrange("(p t) o -> p (t o)", t=LANES))
 
-        w_deal = sb.tile([P, D], I32, name="w_deal", align_bytes=64)
-        nc.vector.tensor_copy(
-            w_deal[:].rearrange("p (t s i) -> p s t i", t=LANES, i=RUN),
-            w_raw[:].rearrange("p (s i t) -> p s t i", t=LANES, i=RUN),
-        )
         ws_deal = sb.tile([P, D], U8, name="ws_deal", align_bytes=64)
         nc.vector.tensor_copy(
             ws_deal[:].rearrange("p (t s) -> p t s", t=LANES),
@@ -71,22 +67,22 @@ def tile_attend_gtshift_pl_kernel(tc, W_words, W_scales, dyT, mu, offs, out_0, o
 
         dy_codes = sb.tile([P, X], I32, name="dy_codes", align_bytes=64)
         dy_scales = sb.tile([P, X], U8, name="dy_scales", align_bytes=64)
-        for c in range(chunks):
-            grouped = sb.tile([P, CHUNK, LANES], BF16, name=f"dy_bf{c}", align_bytes=64)
-            if c == chunks - 1:
-                cut = 80
-                interleave(nc.vector.tensor_copy, grouped[:, :cut, :], dy_raw[c][:, :, :cut])
-                interleave(nc.scalar.copy, grouped[:, cut:, :], dy_raw[c][:, :, cut:])
-            elif c % 2 == 0:
-                interleave(nc.scalar.copy, grouped[:], dy_raw[c][:])
-            else:
-                interleave(nc.vector.tensor_copy, grouped[:], dy_raw[c][:])
-            cols = slice(c * CHUNK, (c + 1) * CHUNK)
+        for (a, b, cut), raw in zip(DY_PIECES, dy_raw):
+            grouped = sb.tile([P, b - a, LANES], BF16, name=f"dy_bf{a}", align_bytes=64)
+            if cut:
+                interleave(nc.vector.tensor_copy, grouped[:, :cut, :], raw[:, :, :cut])
+            interleave(nc.scalar.copy, grouped[:, cut:, :], raw[:, :, cut:])
             nc.vector.quantize_mx(
-                out=dy_codes[:, cols].bitcast(E5M2X4),
-                scales=dy_scales[:, cols],
+                out=dy_codes[:, a:b].bitcast(E5M2X4),
+                scales=dy_scales[:, a:b],
                 in_=grouped[:].rearrange("p c t -> p (c t)"),
             )
+
+        w_deal = sb.tile([P, LANES, P], I32, name="w_deal", align_bytes=64)
+        dealt = w_deal[:].rearrange("p t (s i) -> p s t i", i=RUN)
+        as_loaded = w_raw[:].rearrange("p (s i t) -> p s t i", t=LANES, i=RUN)
+        nc.vector.tensor_copy(dealt[:, :, :1, :], as_loaded[:, :, :1, :])
+        nc.vector.tensor_copy(dealt[:, :, 1:, :], as_loaded[:, :, 1:, :])
 
         one_less = sb.tile([P, LANES], F32, name="one_less")
         nc.vector.tensor_scalar(one_less[:], mu_sb[:], -1.0, 1.0, MULT, ADD)
@@ -96,7 +92,7 @@ def tile_attend_gtshift_pl_kernel(tc, W_words, W_scales, dyT, mu, offs, out_0, o
             bank = ps.tile([P, X], F32, name=f"bank{t}")
             nc.tensor.matmul_mx(
                 out=bank[:],
-                lhsT=w_deal[:, t * P : (t + 1) * P].bitcast(E4M3X4),
+                lhsT=w_deal[:, t, :].bitcast(E4M3X4),
                 lhsT_scale=ws_deal[:, t * P : (t + 1) * P],
                 rhs=dy_codes[:].bitcast(E5M2X4),
                 rhs_scale=dy_scales[:],
@@ -115,13 +111,10 @@ def tile_attend_gtshift_pl_kernel(tc, W_words, W_scales, dyT, mu, offs, out_0, o
             nc.scalar.activation(own[t][:], banks[t][:], COPY, scale=mu_sb[:, t : t + 1])
 
         nc.vector.tensor_copy(u[0][:], banks[0][:])
-        nc.scalar.copy(u[1][:], banks[1][:])
-        scale_own(0)
-        scale_own(1)
-        nc.scalar.copy(u[2][:], banks[2][:])
-        scale_own(2)
-        scale_own(3)
-        nc.scalar.copy(u[3][:], banks[3][:])
+        for t in range(1, LANES):
+            nc.scalar.copy(u[t][:], banks[t][:])
+            scale_own(t - 1)
+        scale_own(LANES - 1)
 
         def gather(t, a, b):
             nc.vector.tensor_copy(nxt[t][:, a:b], u[t][:].indirect(offsets[:, a // PER_COL : b // PER_COL]))
@@ -131,22 +124,28 @@ def tile_attend_gtshift_pl_kernel(tc, W_words, W_scales, dyT, mu, offs, out_0, o
                 y[:, t, a:b], nxt[t][:, a:b], one_less[:, t : t + 1], own[t][:, a:b], MULT, ADD
             )
 
-        for t in range(LANES - 1):
-            gather(t, 0, HALF)
-            gather(t, HALF, X)
-            mix(t, 0, X)
+        for t in range(2):
+            scaled = sb.tile([P, X], F32, name=f"scaled{t}", align_bytes=64)
+            for a in (0, HALF):
+                b = a + HALF
+                gather(t, a, b)
+                nc.gpsimd.tensor_scalar(scaled[:, a:b], nxt[t][:, a:b], one_less[:, t : t + 1], 0.0, MULT, ADD)
+                nc.gpsimd.tensor_tensor(y[:, t, a:b], scaled[:, a:b], own[t][:, a:b], ADD)
             nc.sync.dma_start(y_view[:, t, :], y[:, t, :])
+        gather(2, 0, HALF)
+        gather(2, HALF, X)
 
         y_codes = sb.tile([P, X], I32, name="y_codes", align_bytes=64)
         y_scales = sb.tile([P, X], U8, name="y_scales", align_bytes=64)
         words_view = out_1[0].rearrange("p n t -> p (n t)").bitcast(I32)
-        last = LANES - 1
+        for a in (0, HALF):
+            b = a + HALF
+            gather(3, a, b)
+            mix(2, a, b)
+            mix(3, a, b)
+            nc.sync.dma_start(y_view[:, 2:, a:b], y[:, 2:, a:b])
         for c in range(chunks):
             a, b = c * CHUNK, (c + 1) * CHUNK
-            gather(last, a, b)
-            mix(last, a, b)
-            if c % 2 == 1:
-                nc.sync.dma_start(y_view[:, last, b - HALF : b], y[:, last, b - HALF : b])
             y_bf = sb.tile([P, CHUNK, LANES], BF16, name=f"y_bf{c}", align_bytes=64)
             interleave(nc.vector.tensor_copy if c == chunks - 1 else nc.scalar.copy, y_bf[:], y[:, :, a:b])
             nc.vector.quantize_mx(

@@ -21,7 +21,7 @@ CHUNK = 128
 HALF = 256
 PER_COL = 16
 RUN = 4
-DY_PIECES = ((0, 128, 0), (128, 384, 160), (384, 512, 80))
+DY_PIECES = ((0, 256, 64), (256, 512, 160))
 
 FLOPS = 2 * 512 * 512 * 512
 
@@ -107,14 +107,11 @@ def tile_attend_gtshift_pl_kernel(tc, W_words, W_scales, dyT, mu, offs, out_0, o
         y = sb.tile([P, LANES, X], F32, name="y", align_bytes=64)
         y_view = out_0.rearrange("(p t) x -> p t x", t=LANES)
 
-        def scale_own(t):
-            nc.scalar.activation(own[t][:], banks[t][:], COPY, scale=mu_sb[:, t : t + 1])
+        scaled = [sb.tile([P, X], F32, name=f"scaled{t}", align_bytes=64) for t in range(2)]
+        halves = ((0, HALF), (HALF, X))
 
-        nc.vector.tensor_copy(u[0][:], banks[0][:])
-        for t in range(1, LANES):
-            nc.scalar.copy(u[t][:], banks[t][:])
-            scale_own(t - 1)
-        scale_own(LANES - 1)
+        def scale_own(t, a, b):
+            nc.scalar.activation(own[t][:, a:b], banks[t][:, a:b], COPY, scale=mu_sb[:, t : t + 1])
 
         def gather(t, a, b):
             nc.vector.tensor_copy(nxt[t][:, a:b], u[t][:].indirect(offsets[:, a // PER_COL : b // PER_COL]))
@@ -124,26 +121,37 @@ def tile_attend_gtshift_pl_kernel(tc, W_words, W_scales, dyT, mu, offs, out_0, o
                 y[:, t, a:b], nxt[t][:, a:b], one_less[:, t : t + 1], own[t][:, a:b], MULT, ADD
             )
 
-        for t in range(2):
-            scaled = sb.tile([P, X], F32, name=f"scaled{t}", align_bytes=64)
-            for a in (0, HALF):
-                b = a + HALF
-                gather(t, a, b)
-                nc.gpsimd.tensor_scalar(scaled[:, a:b], nxt[t][:, a:b], one_less[:, t : t + 1], 0.0, MULT, ADD)
-                nc.gpsimd.tensor_tensor(y[:, t, a:b], scaled[:, a:b], own[t][:, a:b], ADD)
-            nc.sync.dma_start(y_view[:, t, :], y[:, t, :])
-        gather(2, 0, HALF)
-        gather(2, HALF, X)
+        nc.vector.tensor_copy(u[0][:], banks[0][:])
+        nc.scalar.copy(u[1][:], banks[1][:])
+        scale_own(0, 0, X)
+        for a, b in halves:
+            gather(0, a, b)
+            nc.gpsimd.tensor_scalar(scaled[0][:, a:b], nxt[0][:, a:b], one_less[:, 0:1], 0.0, MULT, ADD)
+            nc.gpsimd.tensor_tensor(y[:, 0, a:b], scaled[0][:, a:b], own[0][:, a:b], ADD)
+        nc.sync.dma_start(y_view[:, 0, :], y[:, 0, :])
 
-        y_codes = sb.tile([P, X], I32, name="y_codes", align_bytes=64)
-        y_scales = sb.tile([P, X], U8, name="y_scales", align_bytes=64)
-        words_view = out_1[0].rearrange("p n t -> p (n t)").bitcast(I32)
-        for a in (0, HALF):
-            b = a + HALF
+        nc.scalar.copy(u[2][:], banks[2][:])
+        scale_own(1, 0, X)
+        for a, b in halves:
+            gather(1, a, b)
+            nc.scalar.activation(scaled[1][:, a:b], nxt[1][:, a:b], COPY, scale=one_less[:, 1:2])
+            nc.gpsimd.tensor_tensor(y[:, 1, a:b], scaled[1][:, a:b], own[1][:, a:b], ADD)
+        nc.sync.dma_start(y_view[:, 1, :], y[:, 1, :])
+
+        nc.scalar.copy(u[3][:], banks[3][:])
+        for a, b in halves:
+            gather(2, a, b)
+        for a, b in halves:
+            scale_own(2, a, b)
+            scale_own(3, a, b)
             gather(3, a, b)
             mix(2, a, b)
             mix(3, a, b)
             nc.sync.dma_start(y_view[:, 2:, a:b], y[:, 2:, a:b])
+
+        y_codes = sb.tile([P, X], I32, name="y_codes", align_bytes=64)
+        y_scales = sb.tile([P, X], U8, name="y_scales", align_bytes=64)
+        words_view = out_1[0].rearrange("p n t -> p (n t)").bitcast(I32)
         for c in range(chunks):
             a, b = c * CHUNK, (c + 1) * CHUNK
             y_bf = sb.tile([P, CHUNK, LANES], BF16, name=f"y_bf{c}", align_bytes=64)

@@ -103,7 +103,7 @@ def tile_attend_gtshift_pl_kernel(tc, W_words, W_scales, dyT, mu, offs, out_0, o
 
         u = [sb.tile([P, X], F32, name=f"u{t}", align_bytes=64) for t in range(LANES)]
         own = [sb.tile([P, X], F32, name=f"own{t}", align_bytes=64) for t in range(LANES)]
-        nxt = [sb.tile([P, X], F32, name=f"nxt{t}", align_bytes=64) for t in range(LANES)]
+        nxt = [sb.tile([P, X], F32, name=f"nxt{t}", align_bytes=64) for t in range(2)]
         y = sb.tile([P, LANES, X], F32, name="y", align_bytes=64)
         y_view = out_0.rearrange("(p t) x -> p t x", t=LANES)
 
@@ -113,41 +113,56 @@ def tile_attend_gtshift_pl_kernel(tc, W_words, W_scales, dyT, mu, offs, out_0, o
         def scale_own(t, a, b):
             nc.scalar.activation(own[t][:, a:b], banks[t][:, a:b], COPY, scale=mu_sb[:, t : t + 1])
 
-        def gather(t, a, b):
-            nc.vector.tensor_copy(nxt[t][:, a:b], u[t][:].indirect(offsets[:, a // PER_COL : b // PER_COL]))
+        def gather(dst, t, a, b):
+            nc.vector.tensor_copy(dst, u[t][:].indirect(offsets[:, a // PER_COL : b // PER_COL]))
 
-        def mix(t, a, b):
+        def mix(src, t, a, b):
             nc.vector.scalar_tensor_tensor(
-                y[:, t, a:b], nxt[t][:, a:b], one_less[:, t : t + 1], own[t][:, a:b], MULT, ADD
+                y[:, t, a:b], src, one_less[:, t : t + 1], own[t][:, a:b], MULT, ADD
             )
 
-        nc.vector.tensor_copy(u[0][:], banks[0][:])
+        nc.scalar.copy(u[0][:], banks[0][:])
         nc.scalar.copy(u[1][:], banks[1][:])
         scale_own(0, 0, X)
         for a, b in halves:
-            gather(0, a, b)
+            gather(nxt[0][:, a:b], 0, a, b)
             nc.gpsimd.tensor_scalar(scaled[0][:, a:b], nxt[0][:, a:b], one_less[:, 0:1], 0.0, MULT, ADD)
             nc.gpsimd.tensor_tensor(y[:, 0, a:b], scaled[0][:, a:b], own[0][:, a:b], ADD)
         nc.sync.dma_start(y_view[:, 0, :], y[:, 0, :])
 
-        nc.scalar.copy(u[2][:], banks[2][:])
-        scale_own(1, 0, X)
-        for a, b in halves:
-            gather(1, a, b)
+        def scale_next_1(a, b):
             nc.scalar.activation(scaled[1][:, a:b], nxt[1][:, a:b], COPY, scale=one_less[:, 1:2])
-            nc.gpsimd.tensor_tensor(y[:, 1, a:b], scaled[1][:, a:b], own[1][:, a:b], ADD)
-        nc.sync.dma_start(y_view[:, 1, :], y[:, 1, :])
 
-        nc.scalar.copy(u[3][:], banks[3][:])
-        for a, b in halves:
-            gather(2, a, b)
-        for a, b in halves:
-            scale_own(2, a, b)
-            scale_own(3, a, b)
-            gather(3, a, b)
-            mix(2, a, b)
-            mix(3, a, b)
+        def add_1(a, b):
+            nc.gpsimd.tensor_tensor(y[:, 1, a:b], scaled[1][:, a:b], own[1][:, a:b], ADD)
+
+        def gather_and_mix(a, b, name, width):
+            held = sb.tile([P, X], F32, name=name, align_bytes=64)
+            first = {2: 0, 3: HALF}
+            for t in (2, 3):
+                gather(held[:, first[t] : first[t] + HALF], t, a, b)
+            for c in range(0, HALF, width):
+                for t in (2, 3):
+                    mix(held[:, first[t] + c : first[t] + c + width], t, a + c, a + c + width)
             nc.sync.dma_start(y_view[:, 2:, a:b], y[:, 2:, a:b])
+
+        nc.scalar.copy(u[2][:], banks[2][:])
+        for a, b in halves:
+            gather(nxt[1][:, a:b], 1, a, b)
+        scale_own(1, 0, HALF)
+        scale_next_1(0, HALF)
+        add_1(0, HALF)
+        nc.scalar.copy(u[3][:], banks[3][:])
+        scale_own(2, 0, HALF)
+        scale_own(3, 0, HALF)
+        gather_and_mix(0, HALF, "nxt2", HALF)
+        scale_next_1(HALF, X)
+        scale_own(2, HALF, X)
+        scale_own(1, HALF, X)
+        add_1(HALF, X)
+        nc.sync.dma_start(y_view[:, 1, :], y[:, 1, :])
+        scale_own(3, HALF, X)
+        gather_and_mix(HALF, X, "nxt1", CHUNK)
 
         y_codes = sb.tile([P, X], I32, name="y_codes", align_bytes=64)
         y_scales = sb.tile([P, X], U8, name="y_scales", align_bytes=64)

@@ -102,7 +102,8 @@ def tile_attend_gtshift_pl_kernel(tc, W_words, W_scales, dyT, mu, offs, out_0, o
             banks.append(bank)
 
         u = [sb.tile([P, X], F32, name=f"u{t}", align_bytes=64) for t in range(LANES)]
-        own = [sb.tile([P, X], F32, name=f"own{t}", align_bytes=64) for t in range(LANES)]
+        own_0 = sb.tile([P, X], F32, name="own_0", align_bytes=64)
+        own = {}
         nxt = [sb.tile([P, X], F32, name=f"nxt{t}", align_bytes=64) for t in range(2)]
         y = sb.tile([P, LANES, X], F32, name="y", align_bytes=64)
         y_view = out_0.rearrange("(p t) x -> p t x", t=LANES)
@@ -110,31 +111,32 @@ def tile_attend_gtshift_pl_kernel(tc, W_words, W_scales, dyT, mu, offs, out_0, o
         scaled = [sb.tile([P, X], F32, name=f"scaled{t}", align_bytes=64) for t in range(2)]
         halves = ((0, HALF), (HALF, X))
 
-        def scale_own(t, a, b):
-            nc.scalar.activation(own[t][:, a:b], banks[t][:, a:b], COPY, scale=mu_sb[:, t : t + 1])
+        def scale_own(t, a, b, name=None):
+            own[t, a] = sb.tile([P, HALF], F32, name=name or f"own{t}_{a}", align_bytes=64)
+            nc.scalar.activation(own[t, a][:], banks[t][:, a:b], COPY, scale=mu_sb[:, t : t + 1])
 
         def gather(dst, t, a, b):
             nc.vector.tensor_copy(dst, u[t][:].indirect(offsets[:, a // PER_COL : b // PER_COL]))
 
         def mix(src, t, a, b):
             nc.vector.scalar_tensor_tensor(
-                y[:, t, a:b], src, one_less[:, t : t + 1], own[t][:, a:b], MULT, ADD
+                y[:, t, a:b], src, one_less[:, t : t + 1], own[t, a - a % HALF][:, a % HALF : a % HALF + b - a], MULT, ADD
             )
 
         nc.scalar.copy(u[0][:], banks[0][:])
         nc.scalar.copy(u[1][:], banks[1][:])
-        scale_own(0, 0, X)
+        nc.gpsimd.tensor_scalar(own_0[:], u[0][:], mu_sb[:, 0:1], 0.0, MULT, ADD)
         for a, b in halves:
             gather(nxt[0][:, a:b], 0, a, b)
             nc.gpsimd.tensor_scalar(scaled[0][:, a:b], nxt[0][:, a:b], one_less[:, 0:1], 0.0, MULT, ADD)
-            nc.gpsimd.tensor_tensor(y[:, 0, a:b], scaled[0][:, a:b], own[0][:, a:b], ADD)
+            nc.gpsimd.tensor_tensor(y[:, 0, a:b], scaled[0][:, a:b], own_0[:, a:b], ADD)
         nc.sync.dma_start(y_view[:, 0, :], y[:, 0, :])
 
         def scale_next_1(a, b):
             nc.scalar.activation(scaled[1][:, a:b], nxt[1][:, a:b], COPY, scale=one_less[:, 1:2])
 
         def add_1(a, b):
-            nc.gpsimd.tensor_tensor(y[:, 1, a:b], scaled[1][:, a:b], own[1][:, a:b], ADD)
+            nc.gpsimd.tensor_tensor(y[:, 1, a:b], scaled[1][:, a:b], own[1, a][:], ADD)
 
         def gather_and_mix(a, b, name, width):
             held = sb.tile([P, X], F32, name=name, align_bytes=64)
@@ -150,18 +152,18 @@ def tile_attend_gtshift_pl_kernel(tc, W_words, W_scales, dyT, mu, offs, out_0, o
         for a, b in halves:
             gather(nxt[1][:, a:b], 1, a, b)
         scale_own(1, 0, HALF)
+        nc.scalar.copy(u[3][:], banks[3][:])
         scale_next_1(0, HALF)
         add_1(0, HALF)
-        nc.scalar.copy(u[3][:], banks[3][:])
         scale_own(2, 0, HALF)
         scale_own(3, 0, HALF)
         gather_and_mix(0, HALF, "nxt2", HALF)
         scale_next_1(HALF, X)
         scale_own(2, HALF, X)
-        scale_own(1, HALF, X)
+        scale_own(3, HALF, X)
+        scale_own(1, HALF, X, "own2_0")
         add_1(HALF, X)
         nc.sync.dma_start(y_view[:, 1, :], y[:, 1, :])
-        scale_own(3, HALF, X)
         gather_and_mix(HALF, X, "nxt1", CHUNK)
 
         y_codes = sb.tile([P, X], I32, name="y_codes", align_bytes=64)

from contextlib import ExitStack

import concourse.mybir as mybir

F32 = mybir.dt.float32
BF16 = mybir.dt.bfloat16
I32 = mybir.dt.int32
U8 = mybir.dt.uint8
U16 = mybir.dt.uint16
E4M3X4 = mybir.dt.float8_e4m3fn_x4
E5M2X4 = mybir.dt.float8_e5m2_x4
MULT = mybir.AluOpType.mult
ADD = mybir.AluOpType.add
COPY = mybir.ActivationFunctionType.Copy

P = 128
LANES = 4
X = 512
D = 512
CHUNK = 128
HALF = 256
PER_COL = 16
RUN = 4
DY_PIECES = ((0, 256, 64), (256, 512, 160))

FLOPS = 2 * 512 * 512 * 512


def tile_attend_gtshift_pl_kernel(tc, W_words, W_scales, dyT, mu, offs, out_0, out_1, out_2):
    nc = tc.nc
    chunks = X // CHUNK

    def interleave(engine_copy, dst, src):
        engine_copy(
            dst.rearrange("p (c i) t -> p c t i", i=RUN),
            src.rearrange("p t (c i) -> p c t i", i=RUN),
        )

    with ExitStack() as ctx:
        sb = ctx.enter_context(tc.tile_pool(name="sb", bufs=1))
        ps = ctx.enter_context(tc.psum_pool(name="ps", bufs=1))

        offsets = sb.tile([P, X // PER_COL], U16, name="offsets")
        ws_raw = sb.tile([P, D], U8, name="ws_raw", align_bytes=64)
        w_raw = sb.tile([P, D], I32, name="w_raw", align_bytes=64)
        nc.vector.memset(ws_raw[:].bitcast(I32), 0)
        for q in range(4):
            nc.sync.dma_start(
                ws_raw[32 * q : 32 * q + 4, :].bitcast(I32), W_scales[0, 4 * q : 4 * q + 4, :].bitcast(I32)
            )
        dy_view = dyT.rearrange("(p j) x -> p j x", j=LANES)
        dy_raw = []
        for a, b, cut in DY_PIECES:
            raw = sb.tile([P, LANES, b - a], F32, name=f"dy_raw{a}", align_bytes=64)
            nc.sync.dma_start(raw[:], dy_view[:, :, a:b])
            dy_raw.append(raw)
        nc.sync.dma_start(w_raw[:], W_words[0].rearrange("p n t -> p (n t)").bitcast(I32))
        nc.sync.dma_start(offsets[:], offs)
        mu_sb = sb.tile([P, LANES], F32, name="mu_sb")
        nc.sync.dma_start(mu_sb[:], mu.rearrange("(p t) o -> p (t o)", t=LANES))

        ws_deal = sb.tile([P, D], U8, name="ws_deal", align_bytes=64)
        nc.vector.tensor_copy(
            ws_deal[:].rearrange("p (t s) -> p t s", t=LANES),
            ws_raw[:].rearrange("p (s t) -> p t s", t=LANES),
        )

        dy_codes = sb.tile([P, X], I32, name="dy_codes", align_bytes=64)
        dy_scales = sb.tile([P, X], U8, name="dy_scales", align_bytes=64)
        for (a, b, cut), raw in zip(DY_PIECES, dy_raw):
            grouped = sb.tile([P, b - a, LANES], BF16, name=f"dy_bf{a}", align_bytes=64)
            if cut:
                interleave(nc.vector.tensor_copy, grouped[:, :cut, :], raw[:, :, :cut])
            interleave(nc.scalar.copy, grouped[:, cut:, :], raw[:, :, cut:])
            nc.vector.quantize_mx(
                out=dy_codes[:, a:b].bitcast(E5M2X4),
                scales=dy_scales[:, a:b],
                in_=grouped[:].rearrange("p c t -> p (c t)"),
            )

        w_deal = sb.tile([P, LANES, P], I32, name="w_deal", align_bytes=64)
        dealt = w_deal[:].rearrange("p t (s i) -> p s t i", i=RUN)
        as_loaded = w_raw[:].rearrange("p (s i t) -> p s t i", t=LANES, i=RUN)
        nc.vector.tensor_copy(dealt[:, :, :1, :], as_loaded[:, :, :1, :])
        nc.vector.tensor_copy(dealt[:, :, 1:, :], as_loaded[:, :, 1:, :])

        one_less = sb.tile([P, LANES], F32, name="one_less")
        nc.vector.tensor_scalar(one_less[:], mu_sb[:], -1.0, 1.0, MULT, ADD)

        banks = []
        for t in range(LANES):
            bank = ps.tile([P, X], F32, name=f"bank{t}")
            nc.tensor.matmul_mx(
                out=bank[:],
                lhsT=w_deal[:, t, :].bitcast(E4M3X4),
                lhsT_scale=ws_deal[:, t * P : (t + 1) * P],
                rhs=dy_codes[:].bitcast(E5M2X4),
                rhs_scale=dy_scales[:],
                start=True,
                stop=True,
            )
            banks.append(bank)

        u = [sb.tile([P, X], F32, name=f"u{t}", align_bytes=64) for t in range(LANES)]
        own_0 = sb.tile([P, X], F32, name="own_0", align_bytes=64)
        own = {}
        nxt = [sb.tile([P, X], F32, name=f"nxt{t}", align_bytes=64) for t in range(2)]
        y = sb.tile([P, LANES, X], F32, name="y", align_bytes=64)
        y_view = out_0.rearrange("(p t) x -> p t x", t=LANES)

        scaled = [sb.tile([P, X], F32, name=f"scaled{t}", align_bytes=64) for t in range(2)]
        halves = ((0, HALF), (HALF, X))

        def scale_own(t, a, b, name=None):
            own[t, a] = sb.tile([P, HALF], F32, name=name or f"own{t}_{a}", align_bytes=64)
            nc.scalar.activation(own[t, a][:], banks[t][:, a:b], COPY, scale=mu_sb[:, t : t + 1])

        def gather(dst, t, a, b):
            nc.vector.tensor_copy(dst, u[t][:].indirect(offsets[:, a // PER_COL : b // PER_COL]))

        def mix(src, t, a, b):
            nc.vector.scalar_tensor_tensor(
                y[:, t, a:b], src, one_less[:, t : t + 1], own[t, a - a % HALF][:, a % HALF : a % HALF + b - a], MULT, ADD
            )

        nc.scalar.copy(u[0][:], banks[0][:])
        nc.scalar.copy(u[1][:], banks[1][:])
        nc.gpsimd.tensor_scalar(own_0[:], u[0][:], mu_sb[:, 0:1], 0.0, MULT, ADD)
        for a, b in halves:
            gather(nxt[0][:, a:b], 0, a, b)
            nc.gpsimd.tensor_scalar(scaled[0][:, a:b], nxt[0][:, a:b], one_less[:, 0:1], 0.0, MULT, ADD)
            nc.gpsimd.tensor_tensor(y[:, 0, a:b], scaled[0][:, a:b], own_0[:, a:b], ADD)
        nc.sync.dma_start(y_view[:, 0, :], y[:, 0, :])

        def scale_next_1(a, b):
            nc.scalar.activation(scaled[1][:, a:b], nxt[1][:, a:b], COPY, scale=one_less[:, 1:2])

        def add_1(a, b):
            nc.gpsimd.tensor_tensor(y[:, 1, a:b], scaled[1][:, a:b], own[1, a][:], ADD)

        def gather_and_mix(a, b, name, width):
            held = sb.tile([P, X], F32, name=name, align_bytes=64)
            first = {2: 0, 3: HALF}
            for t in (2, 3):
                gather(held[:, first[t] : first[t] + HALF], t, a, b)
            for c in range(0, HALF, width):
                for t in (2, 3):
                    mix(held[:, first[t] + c : first[t] + c + width], t, a + c, a + c + width)
            nc.sync.dma_start(y_view[:, 2:, a:b], y[:, 2:, a:b])

        nc.scalar.copy(u[2][:], banks[2][:])
        for a, b in halves:
            gather(nxt[1][:, a:b], 1, a, b)
        scale_own(1, 0, HALF)
        nc.scalar.copy(u[3][:], banks[3][:])
        scale_next_1(0, HALF)
        add_1(0, HALF)
        scale_own(2, 0, HALF)
        scale_own(3, 0, HALF)
        gather_and_mix(0, HALF, "nxt2", HALF)
        scale_next_1(HALF, X)
        scale_own(2, HALF, X)
        scale_own(3, HALF, X)
        scale_own(1, HALF, X, "own2_0")
        add_1(HALF, X)
        nc.sync.dma_start(y_view[:, 1, :], y[:, 1, :])
        gather_and_mix(HALF, X, "nxt1", CHUNK)

        y_codes = sb.tile([P, X], I32, name="y_codes", align_bytes=64)
        y_scales = sb.tile([P, X], U8, name="y_scales", align_bytes=64)
        words_view = out_1[0].rearrange("p n t -> p (n t)").bitcast(I32)
        for c in range(chunks):
            a, b = c * CHUNK, (c + 1) * CHUNK
            y_bf = sb.tile([P, CHUNK, LANES], BF16, name=f"y_bf{c}", align_bytes=64)
            interleave(nc.vector.tensor_copy if c == chunks - 1 else nc.scalar.copy, y_bf[:], y[:, :, a:b])
            nc.vector.quantize_mx(
                out=y_codes[:, a:b].bitcast(E4M3X4),
                scales=y_scales[:, a:b],
                in_=y_bf[:].rearrange("p c t -> p (c t)"),
            )
            if c % 2 == 1:
                nc.sync.dma_start(words_view[:, b - HALF : b], y_codes[:, b - HALF : b])
        for q in range(4):
            queue = nc.scalar if q % 2 == 0 else nc.sync
            queue.dma_start(
                out_2[0, 4 * q : 4 * q + 4, :].bitcast(I32), y_scales[32 * q : 32 * q + 4, :].bitcast(I32)
            )
